import numpy as np
import ml_dtypes


def mxq(x, axis, fmt="e4m3"):
    dtype, down = {"e4m3": (ml_dtypes.float8_e4m3fn, 7), "e5m2": (ml_dtypes.float8_e5m2, 14)}[fmt]
    v = np.moveaxis(np.asarray(x, np.float32).astype(ml_dtypes.bfloat16).astype(np.float64), axis, -1)
    blocks = v.reshape(v.shape[:-1] + (-1, 32))
    amax = np.abs(blocks).max(-1, keepdims=True)
    byte = np.maximum(np.where(amax > 0, np.frexp(amax)[1] - 1 + 127, 0) - down, 1)
    scale = np.exp2(byte - 127.0)
    codes = (blocks / scale).astype(np.float32).astype(dtype).astype(np.float64)
    return np.moveaxis((codes * scale).reshape(v.shape), -1, axis)


WIDE = False


def mx_kscale(k):
    if not WIDE:
        return np.ones(k)
    levels = np.array([10, -10, 5, -5, 0])
    if k % 512:
        return np.exp2(np.random.permutation(np.resize(levels, k // 32))).repeat(32)
    a = np.empty((k // 512, 16))
    for p in range(k // 512):
        a[p, :8] = np.random.permutation(np.resize(levels, 8))
        for g in range(8):
            far = levels[np.abs(levels - a[p, g]) >= 10]
            a[p, g + 8] = far[np.random.randint(len(far))]
    return np.exp2(a.ravel()).repeat(32)


def f64(x):
    return np.asarray(x).astype(np.float64)


def striped(idx):
    return np.tile(idx.reshape(-1, 16).T, (8, 1)).astype(np.uint16)


def unstriped(offs):
    return offs[:16].T.reshape(-1).astype(np.int64)


def sigmoid(v):
    return 1.0 / (1.0 + np.exp(-np.maximum(v, -700.0)))


K, T, S, V, N = 512, 2048, 512, 256, 128


def setup_inputs():
    n = np.random.standard_normal
    s = mx_kscale(K)[:, None]
    return {
        "xT": (n((K, T)) * s).astype(np.float32),
        "w1": (n((K, N)) / np.sqrt(K) / s).astype(np.float32),
        "offs": striped(np.random.permutation(T)[:S]),
        "win": striped(np.random.permutation(S)[:V]),
        "lose": striped(np.random.permutation(S)[:V]),
    }


def reference(xT, w1, offs, win, lose):
    xq = mxq(f64(xT)[:, unstriped(offs)], 0, "e4m3")
    y = mxq(f64(w1), 0, "e4m3").T @ xq
    return sigmoid(y[:, unstriped(win)] - y[:, unstriped(lose)])

@@ -1,0 +1,101 @@
+from contextlib import ExitStack
+
+import concourse.mybir as mybir
+
+K, T, S, V, N = 512, 2048, 512, 256, 128
+FLOPS = 2 * K * S * N
+
+F32 = mybir.dt.float32
+BF16 = mybir.dt.bfloat16
+U32 = mybir.dt.uint32
+U16 = mybir.dt.uint16
+U8 = mybir.dt.uint8
+FP8X4 = mybir.dt.float8_e4m3fn_x4
+ACT = mybir.ActivationFunctionType
+ALU = mybir.AluOpType
+
+P = 128
+PACK = 4
+LANES = 16
+HALF = S // 2
+QUARTER = S // 4
+PAIR_HALF = V // 2
+
+
+def tile_picked_ranknet_sigmoid_e_kernel(tc, xT, w1, offs, win, lose, out):
+    nc = tc.nc
+    with ExitStack() as ctx:
+        keep = ctx.enter_context(tc.tile_pool(name="keep", bufs=1))
+        psum = ctx.enter_context(tc.psum_pool(name="psum", bufs=1))
+
+        offs_sb = keep.tile([P, S // LANES], U16, name="offs_sb")
+        win_sb = keep.tile([P, V // LANES], U16, name="win_sb")
+        lose_sb = keep.tile([P, V // LANES], U16, name="lose_sb")
+        planes = [keep.tile([P, T], F32, name=f"plane{j}") for j in range(PACK)]
+        w_raw = keep.tile([P, PACK, N], F32, name="w_raw")
+
+        x_rows = xT.rearrange("(p j) t -> p j t", j=PACK)
+        nc.sync.dma_start(planes[0][:], x_rows[:, 0, :])
+        nc.sync.dma_start(offs_sb[:], offs)
+        for j in range(1, PACK):
+            nc.sync.dma_start(planes[j][:], x_rows[:, j, :])
+        nc.sync.dma_start(w_raw[:], w1.rearrange("(p j) n -> p j n", j=PACK))
+        nc.sync.dma_start(win_sb[:], win)
+        nc.sync.dma_start(lose_sb[:], lose)
+
+        warm_in = keep.tile([P, 1], F32, name="warm_in")
+        warm_out = keep.tile([P, 1], F32, name="warm_out")
+        nc.gpsimd.memset(warm_in[:], 0.0)
+        nc.scalar.activation(warm_out[:], warm_in[:], ACT.Sigmoid)
+
+        picked = [keep.tile([P, HALF * PACK], BF16, name=f"picked{h}", align_bytes=64) for h in range(2)]
+        for j in range(PACK):
+            for h in range(2):
+                cols = slice(h * HALF // LANES, (h + 1) * HALF // LANES)
+                nc.vector.tensor_copy(
+                    picked[h][:].rearrange("p (s j) -> p s j", j=PACK)[:, :, j],
+                    planes[j][:].indirect(offs_sb[:, cols]),
+                )
+
+        w_grouped = keep.tile([P, N * PACK], BF16, name="w_grouped", align_bytes=64)
+        nc.scalar.copy(w_grouped[:].rearrange("p (n j) -> p n j", j=PACK), w_raw[:].rearrange("p j n -> p n j"))
+        w_codes = keep.tile([P, N], U32, name="w_codes", align_bytes=64)
+        w_scales = keep.tile([P, N], U8, name="w_scales", align_bytes=64)
+        nc.vector.quantize_mx(out=w_codes[:].bitcast(FP8X4), scales=w_scales[:], in_=w_grouped[:])
+
+        scores = keep.tile([P, S], F32, name="scores")
+        pieces = [(0, 0, HALF), (1, 0, QUARTER), (1, QUARTER, QUARTER)]
+        for i, (h, first, width) in enumerate(pieces):
+            codes = keep.tile([P, width], U32, name=f"x_codes{i}", align_bytes=64)
+            scales = keep.tile([P, width], U8, name=f"x_scales{i}", align_bytes=64)
+            nc.vector.quantize_mx(
+                out=codes[:].bitcast(FP8X4),
+                scales=scales[:],
+                in_=picked[h][:, first * PACK : (first + width) * PACK],
+            )
+            acc = psum.tile([P, width], F32, name=f"acc{i}")
+            nc.tensor.matmul_mx(
+                out=acc[:],
+                lhsT=w_codes[:].bitcast(FP8X4),
+                lhsT_scale=w_scales[:],
+                rhs=codes[:].bitcast(FP8X4),
+                rhs_scale=scales[:],
+                start=True,
+                stop=True,
+            )
+            dst = scores[:, h * HALF + first : h * HALF + first + width]
+            if i == len(pieces) - 1:
+                nc.vector.tensor_copy(dst, acc[:])
+            else:
+                nc.scalar.copy(dst, acc[:])
+
+        winners = [keep.tile([P, PAIR_HALF], F32, name=f"winners{h}") for h in range(2)]
+        gaps = [keep.tile([P, PAIR_HALF], F32, name=f"gaps{h}") for h in range(2)]
+        probs = [keep.tile([P, PAIR_HALF], F32, name=f"probs{h}") for h in range(2)]
+        pair_cols = [slice(h * PAIR_HALF // LANES, (h + 1) * PAIR_HALF // LANES) for h in range(2)]
+        for h in range(2):
+            nc.vector.tensor_copy(winners[h][:], scores[:].indirect(win_sb[:, pair_cols[h]]))
+        for h in range(2):
+            nc.vector.tensor_tensor(gaps[h][:], scores[:].indirect(lose_sb[:, pair_cols[h]]), winners[h][:], ALU.subtract)
+            nc.scalar.activation(probs[h][:], gaps[h][:], ACT.Sigmoid, scale=-1.0)
+            nc.sync.dma_start(out[:, h * PAIR_HALF : (h + 1) * PAIR_HALF], probs[h][:])

@@ -19,7 +19,7 @@ PACK = 4
 LANES = 16
 HALF = S // 2
 QUARTER = S // 4
-PAIR_HALF = V // 2
+PAIRS_FIRST = 192
 
 
 def tile_picked_ranknet_sigmoid_e_kernel(tc, xT, w1, offs, win, lose, out):
@@ -32,7 +32,7 @@ def tile_picked_ranknet_sigmoid_e_kernel(tc, xT, w1, offs, win, lose, out):
         win_sb = keep.tile([P, V // LANES], U16, name="win_sb")
         lose_sb = keep.tile([P, V // LANES], U16, name="lose_sb")
         planes = [keep.tile([P, T], F32, name=f"plane{j}") for j in range(PACK)]
-        w_raw = keep.tile([P, PACK, N], F32, name="w_raw")
+        w_raw = keep.tile([P, PACK, N], F32, name="w_raw", tag="w_then_codes", align_bytes=64)
 
         x_rows = xT.rearrange("(p j) t -> p j t", j=PACK)
         nc.sync.dma_start(planes[0][:], x_rows[:, 0, :])
@@ -63,13 +63,14 @@ def tile_picked_ranknet_sigmoid_e_kernel(tc, xT, w1, offs, win, lose, out):
         w_scales = keep.tile([P, N], U8, name="w_scales", align_bytes=64)
         nc.vector.quantize_mx(out=w_codes[:].bitcast(FP8X4), scales=w_scales[:], in_=w_grouped[:])
 
+        x_codes = keep.tile([P, S], U32, name="x_codes", tag="w_then_codes", align_bytes=64)
         scores = keep.tile([P, S], F32, name="scores")
-        pieces = [(0, 0, HALF), (1, 0, QUARTER), (1, QUARTER, QUARTER)]
+        pieces = [(0, 0, QUARTER), (0, QUARTER, QUARTER), (1, 0, QUARTER), (1, QUARTER, QUARTER)]
         for i, (h, first, width) in enumerate(pieces):
-            codes = keep.tile([P, width], U32, name=f"x_codes{i}", align_bytes=64)
+            codes = x_codes[:, i * width : (i + 1) * width]
             scales = keep.tile([P, width], U8, name=f"x_scales{i}", align_bytes=64)
             nc.vector.quantize_mx(
-                out=codes[:].bitcast(FP8X4),
+                out=codes.bitcast(FP8X4),
                 scales=scales[:],
                 in_=picked[h][:, first * PACK : (first + width) * PACK],
             )
@@ -78,24 +79,24 @@ def tile_picked_ranknet_sigmoid_e_kernel(tc, xT, w1, offs, win, lose, out):
                 out=acc[:],
                 lhsT=w_codes[:].bitcast(FP8X4),
                 lhsT_scale=w_scales[:],
-                rhs=codes[:].bitcast(FP8X4),
+                rhs=codes.bitcast(FP8X4),
                 rhs_scale=scales[:],
                 start=True,
                 stop=True,
             )
             dst = scores[:, h * HALF + first : h * HALF + first + width]
-            if i == len(pieces) - 1:
+            if i == len(pieces) - 2:
                 nc.vector.tensor_copy(dst, acc[:])
             else:
                 nc.scalar.copy(dst, acc[:])
 
-        winners = [keep.tile([P, PAIR_HALF], F32, name=f"winners{h}") for h in range(2)]
-        gaps = [keep.tile([P, PAIR_HALF], F32, name=f"gaps{h}") for h in range(2)]
-        probs = [keep.tile([P, PAIR_HALF], F32, name=f"probs{h}") for h in range(2)]
-        pair_cols = [slice(h * PAIR_HALF // LANES, (h + 1) * PAIR_HALF // LANES) for h in range(2)]
-        for h in range(2):
-            nc.vector.tensor_copy(winners[h][:], scores[:].indirect(win_sb[:, pair_cols[h]]))
-        for h in range(2):
-            nc.vector.tensor_tensor(gaps[h][:], scores[:].indirect(lose_sb[:, pair_cols[h]]), winners[h][:], ALU.subtract)
+        spans = [(0, PAIRS_FIRST), (PAIRS_FIRST, V)]
+        winners = [keep.tile([P, b - a], F32, name=f"winners{a}") for a, b in spans]
+        gaps = [keep.tile([P, b - a], F32, name=f"gaps{a}") for a, b in spans]
+        probs = [keep.tile([P, b - a], F32, name=f"probs{a}") for a, b in spans]
+        for h, (a, b) in enumerate(spans):
+            nc.vector.tensor_copy(winners[h][:], scores[:].indirect(win_sb[:, a // LANES : b // LANES]))
+        for h, (a, b) in enumerate(spans):
+            nc.vector.tensor_tensor(gaps[h][:], scores[:].indirect(lose_sb[:, a // LANES : b // LANES]), winners[h][:], ALU.subtract)
             nc.scalar.activation(probs[h][:], gaps[h][:], ACT.Sigmoid, scale=-1.0)
-            nc.sync.dma_start(out[:, h * PAIR_HALF : (h + 1) * PAIR_HALF], probs[h][:])
+            (nc.sync if h == 0 else nc.scalar).dma_start(out[:, a:b], probs[h][:])

@@ -19,7 +19,7 @@ PACK = 4
 LANES = 16
 HALF = S // 2
 QUARTER = S // 4
-PAIRS_FIRST = 192
+PAIRS_FIRST = 128
 
 
 def tile_picked_ranknet_sigmoid_e_kernel(tc, xT, w1, offs, win, lose, out):
@@ -99,4 +99,4 @@ def tile_picked_ranknet_sigmoid_e_kernel(tc, xT, w1, offs, win, lose, out):
         for h, (a, b) in enumerate(spans):
             nc.vector.tensor_tensor(gaps[h][:], scores[:].indirect(lose_sb[:, a // LANES : b // LANES]), winners[h][:], ALU.subtract)
             nc.scalar.activation(probs[h][:], gaps[h][:], ACT.Sigmoid, scale=-1.0)
-            (nc.sync if h == 0 else nc.scalar).dma_start(out[:, a:b], probs[h][:])
+            nc.sync.dma_start(out[:, a:b], probs[h][:])

@@ -49,7 +49,15 @@ def tile_picked_ranknet_sigmoid_e_kernel(tc, xT, w1, offs, win, lose, out):
         nc.scalar.activation(warm_out[:], warm_in[:], ACT.Sigmoid)
 
         picked = [keep.tile([P, HALF * PACK], BF16, name=f"picked{h}", align_bytes=64) for h in range(2)]
-        for j in range(PACK):
+        flat = keep.tile([P, 2, S], BF16, name="flat")
+        for j in range(2):
+            nc.vector.tensor_copy(flat[:, j, :], planes[j][:].indirect(offs_sb[:]))
+        for h in range(2):
+            nc.scalar.copy(
+                picked[h][:].rearrange("p (s j) -> p s j", j=PACK)[:, :, 0:2],
+                flat[:, :, h * HALF : (h + 1) * HALF].rearrange("p j s -> p s j"),
+            )
+        for j in range(2, PACK):
             for h in range(2):
                 cols = slice(h * HALF // LANES, (h + 1) * HALF // LANES)
                 nc.vector.tensor_copy(

@@ -20,6 +20,7 @@ LANES = 16
 HALF = S // 2
 QUARTER = S // 4
 PAIRS_FIRST = 128
+LINE = 4
 
 
 def tile_picked_ranknet_sigmoid_e_kernel(tc, xT, w1, offs, win, lose, out):
@@ -66,22 +67,27 @@ def tile_picked_ranknet_sigmoid_e_kernel(tc, xT, w1, offs, win, lose, out):
                 )
 
         w_grouped = keep.tile([P, N * PACK], BF16, name="w_grouped", align_bytes=64)
-        nc.scalar.copy(w_grouped[:].rearrange("p (n j) -> p n j", j=PACK), w_raw[:].rearrange("p j n -> p n j"))
+        nc.scalar.copy(
+            w_grouped[:].rearrange("p (c i j) -> p c j i", i=LINE, j=PACK),
+            w_raw[:].rearrange("p j (c i) -> p c j i", i=LINE),
+        )
         w_codes = keep.tile([P, N], U32, name="w_codes", align_bytes=64)
         w_scales = keep.tile([P, N], U8, name="w_scales", align_bytes=64)
-        nc.vector.quantize_mx(out=w_codes[:].bitcast(FP8X4), scales=w_scales[:], in_=w_grouped[:])
 
+        first_codes = keep.tile([P, QUARTER], U32, name="first_codes", align_bytes=64)
         x_codes = keep.tile([P, S], U32, name="x_codes", tag="w_then_codes", align_bytes=64)
         scores = keep.tile([P, S], F32, name="scores")
         pieces = [(0, 0, QUARTER), (0, QUARTER, QUARTER), (1, 0, QUARTER), (1, QUARTER, QUARTER)]
         for i, (h, first, width) in enumerate(pieces):
-            codes = x_codes[:, i * width : (i + 1) * width]
+            codes = x_codes[:, i * width : (i + 1) * width] if i else first_codes[:]
             scales = keep.tile([P, width], U8, name=f"x_scales{i}", align_bytes=64)
             nc.vector.quantize_mx(
                 out=codes.bitcast(FP8X4),
                 scales=scales[:],
                 in_=picked[h][:, first * PACK : (first + width) * PACK],
             )
+            if i == 0:
+                nc.vector.quantize_mx(out=w_codes[:].bitcast(FP8X4), scales=w_scales[:], in_=w_grouped[:])
             acc = psum.tile([P, width], F32, name=f"acc{i}")
             nc.tensor.matmul_mx(
                 out=acc[:],
@@ -93,10 +99,7 @@ def tile_picked_ranknet_sigmoid_e_kernel(tc, xT, w1, offs, win, lose, out):
                 stop=True,
             )
             dst = scores[:, h * HALF + first : h * HALF + first + width]
-            if i == len(pieces) - 2:
-                nc.vector.tensor_copy(dst, acc[:])
-            else:
-                nc.scalar.copy(dst, acc[:])
+            nc.scalar.copy(dst, acc[:])
 
         spans = [(0, PAIRS_FIRST), (PAIRS_FIRST, V)]
         winners = [keep.tile([P, b - a], F32, name=f"winners{a}") for a, b in spans]

@@ -19,8 +19,9 @@ PACK = 4
 LANES = 16
 HALF = S // 2
 QUARTER = S // 4
-PAIRS_FIRST = 128
 LINE = 4
+STORE_CUT = V // 2
+STEP_CUT = 3 * V // 4
 
 
 def tile_picked_ranknet_sigmoid_e_kernel(tc, xT, w1, offs, win, lose, out):
@@ -46,7 +47,7 @@ def tile_picked_ranknet_sigmoid_e_kernel(tc, xT, w1, offs, win, lose, out):
 
         warm_in = keep.tile([P, 1], F32, name="warm_in")
         warm_out = keep.tile([P, 1], F32, name="warm_out")
-        nc.gpsimd.memset(warm_in[:], 0.0)
+        nc.vector.memset(warm_in[:], 0.0)
         nc.scalar.activation(warm_out[:], warm_in[:], ACT.Sigmoid)
 
         picked = [keep.tile([P, HALF * PACK], BF16, name=f"picked{h}", align_bytes=64) for h in range(2)]
@@ -60,10 +61,10 @@ def tile_picked_ranknet_sigmoid_e_kernel(tc, xT, w1, offs, win, lose, out):
             )
         for j in range(2, PACK):
             for h in range(2):
-                cols = slice(h * HALF // LANES, (h + 1) * HALF // LANES)
+                entries = slice(h * HALF // LANES, (h + 1) * HALF // LANES)
                 nc.vector.tensor_copy(
                     picked[h][:].rearrange("p (s j) -> p s j", j=PACK)[:, :, j],
-                    planes[j][:].indirect(offs_sb[:, cols]),
+                    planes[j][:].indirect(offs_sb[:, entries]),
                 )
 
         w_grouped = keep.tile([P, N * PACK], BF16, name="w_grouped", align_bytes=64)
@@ -75,20 +76,21 @@ def tile_picked_ranknet_sigmoid_e_kernel(tc, xT, w1, offs, win, lose, out):
         w_scales = keep.tile([P, N], U8, name="w_scales", align_bytes=64)
 
         first_codes = keep.tile([P, QUARTER], U32, name="first_codes", align_bytes=64)
-        x_codes = keep.tile([P, S], U32, name="x_codes", tag="w_then_codes", align_bytes=64)
+        later_codes = keep.tile([P, S], U32, name="later_codes", tag="w_then_codes", align_bytes=64)
         scores = keep.tile([P, S], F32, name="scores")
-        pieces = [(0, 0, QUARTER), (0, QUARTER, QUARTER), (1, 0, QUARTER), (1, QUARTER, QUARTER)]
-        for i, (h, first, width) in enumerate(pieces):
-            codes = x_codes[:, i * width : (i + 1) * width] if i else first_codes[:]
-            scales = keep.tile([P, width], U8, name=f"x_scales{i}", align_bytes=64)
+        for q in range(S // QUARTER):
+            h, first = divmod(q * QUARTER, HALF)
+            documents = slice(q * QUARTER, (q + 1) * QUARTER)
+            codes = later_codes[:, documents] if q else first_codes[:]
+            scales = keep.tile([P, QUARTER], U8, name=f"x_scales{q}", align_bytes=64)
             nc.vector.quantize_mx(
                 out=codes.bitcast(FP8X4),
                 scales=scales[:],
-                in_=picked[h][:, first * PACK : (first + width) * PACK],
+                in_=picked[h][:, first * PACK : (first + QUARTER) * PACK],
             )
-            if i == 0:
+            if q == 0:
                 nc.vector.quantize_mx(out=w_codes[:].bitcast(FP8X4), scales=w_scales[:], in_=w_grouped[:])
-            acc = psum.tile([P, width], F32, name=f"acc{i}")
+            acc = psum.tile([P, QUARTER], F32, name=f"acc{q}")
             nc.tensor.matmul_mx(
                 out=acc[:],
                 lhsT=w_codes[:].bitcast(FP8X4),
@@ -98,16 +100,18 @@ def tile_picked_ranknet_sigmoid_e_kernel(tc, xT, w1, offs, win, lose, out):
                 start=True,
                 stop=True,
             )
-            dst = scores[:, h * HALF + first : h * HALF + first + width]
-            nc.scalar.copy(dst, acc[:])
+            nc.scalar.copy(scores[:, documents], acc[:])
 
-        spans = [(0, PAIRS_FIRST), (PAIRS_FIRST, V)]
-        winners = [keep.tile([P, b - a], F32, name=f"winners{a}") for a, b in spans]
-        gaps = [keep.tile([P, b - a], F32, name=f"gaps{a}") for a, b in spans]
-        probs = [keep.tile([P, b - a], F32, name=f"probs{a}") for a, b in spans]
-        for h, (a, b) in enumerate(spans):
-            nc.vector.tensor_copy(winners[h][:], scores[:].indirect(win_sb[:, a // LANES : b // LANES]))
-        for h, (a, b) in enumerate(spans):
-            nc.vector.tensor_tensor(gaps[h][:], scores[:].indirect(lose_sb[:, a // LANES : b // LANES]), winners[h][:], ALU.subtract)
-            nc.scalar.activation(probs[h][:], gaps[h][:], ACT.Sigmoid, scale=-1.0)
-            nc.sync.dma_start(out[:, a:b], probs[h][:])
+        stores = [(0, STORE_CUT), (STORE_CUT, V)]
+        steps = [[(0, STORE_CUT)], [(STORE_CUT, STEP_CUT), (STEP_CUT, V)]]
+        winners = keep.tile([P, V], F32, name="winners")
+        gaps = keep.tile([P, V], F32, name="gaps")
+        probs = keep.tile([P, V], F32, name="probs")
+        for a, b in stores:
+            nc.vector.tensor_copy(winners[:, a:b], scores[:].indirect(win_sb[:, a // LANES : b // LANES]))
+        for (a, b), store_steps in zip(stores, steps):
+            for c, d in store_steps:
+                losers = scores[:].indirect(lose_sb[:, c // LANES : d // LANES])
+                nc.vector.tensor_tensor(gaps[:, c:d], losers, winners[:, c:d], ALU.subtract)
+                nc.scalar.activation(probs[:, c:d], gaps[:, c:d], ACT.Sigmoid, scale=-1.0)
+            nc.sync.dma_start(out[:, a:b], probs[:, a:b])

@@ -19,6 +19,8 @@ PACK = 4
 LANES = 16
 HALF = S // 2
 QUARTER = S // 4
+W_CUT = 56
+EIGHTH = S // 8
 LINE = 4
 STORE_CUT = V // 2
 STEP_CUT = 3 * V // 4
@@ -28,19 +30,22 @@ def tile_picked_ranknet_sigmoid_e_kernel(tc, xT, w1, offs, win, lose, out):
     nc = tc.nc
     with ExitStack() as ctx:
         keep = ctx.enter_context(tc.tile_pool(name="keep", bufs=1))
+        reuse = ctx.enter_context(tc.tile_pool(name="reuse", bufs=1))
         psum = ctx.enter_context(tc.psum_pool(name="psum", bufs=1))
 
         offs_sb = keep.tile([P, S // LANES], U16, name="offs_sb")
         win_sb = keep.tile([P, V // LANES], U16, name="win_sb")
         lose_sb = keep.tile([P, V // LANES], U16, name="lose_sb")
         planes = [keep.tile([P, T], F32, name=f"plane{j}") for j in range(PACK)]
-        w_raw = keep.tile([P, PACK, N], F32, name="w_raw", tag="w_then_codes", align_bytes=64)
+        w_raw = reuse.tile([P, PACK, N], F32, name="w_raw", align_bytes=64, offset=512)
 
         x_rows = xT.rearrange("(p j) t -> p j t", j=PACK)
-        nc.sync.dma_start(planes[0][:], x_rows[:, 0, :])
-        nc.sync.dma_start(offs_sb[:], offs)
-        for j in range(1, PACK):
-            nc.sync.dma_start(planes[j][:], x_rows[:, j, :])
+        for j in range(PACK):
+            cuts = [0, T // 2, 3 * T // 4, T] if j < PACK - 1 else [0, T]
+            for a, b in zip(cuts, cuts[1:]):
+                nc.sync.dma_start(planes[j][:, a:b], x_rows[:, j, a:b])
+            if j == 0:
+                nc.sync.dma_start(offs_sb[:], offs)
         nc.sync.dma_start(w_raw[:], w1.rearrange("(p j) n -> p j n", j=PACK))
         nc.sync.dma_start(win_sb[:], win)
         nc.sync.dma_start(lose_sb[:], lose)
@@ -50,46 +55,59 @@ def tile_picked_ranknet_sigmoid_e_kernel(tc, xT, w1, offs, win, lose, out):
         nc.vector.memset(warm_in[:], 0.0)
         nc.scalar.activation(warm_out[:], warm_in[:], ACT.Sigmoid)
 
-        picked = [keep.tile([P, HALF * PACK], BF16, name=f"picked{h}", align_bytes=64) for h in range(2)]
-        flat = keep.tile([P, 2, S], BF16, name="flat")
-        for j in range(2):
-            nc.vector.tensor_copy(flat[:, j, :], planes[j][:].indirect(offs_sb[:]))
-        for h in range(2):
-            nc.scalar.copy(
-                picked[h][:].rearrange("p (s j) -> p s j", j=PACK)[:, :, 0:2],
-                flat[:, :, h * HALF : (h + 1) * HALF].rearrange("p j s -> p s j"),
+        direct = keep.tile([P, HALF * PACK], BF16, name="direct", align_bytes=64)
+        pairs = keep.tile([P, 2, HALF * 2], BF16, name="pairs")
+        first_half = offs_sb[:, : HALF // LANES]
+        second_half = offs_sb[:, HALF // LANES :]
+        for j in range(PACK):
+            u, e = divmod(j, 2)
+            nc.vector.tensor_copy(
+                pairs[:, u, :].rearrange("p (s e) -> p s e", e=2)[:, :, e], planes[j][:].indirect(second_half)
             )
-        for j in range(2, PACK):
-            for h in range(2):
-                entries = slice(h * HALF // LANES, (h + 1) * HALF // LANES)
-                nc.vector.tensor_copy(
-                    picked[h][:].rearrange("p (s j) -> p s j", j=PACK)[:, :, j],
-                    planes[j][:].indirect(offs_sb[:, entries]),
-                )
+            nc.vector.tensor_copy(
+                direct[:].rearrange("p (s j) -> p s j", j=PACK)[:, :, j], planes[j][:].indirect(first_half)
+            )
 
         w_grouped = keep.tile([P, N * PACK], BF16, name="w_grouped", align_bytes=64)
-        nc.scalar.copy(
-            w_grouped[:].rearrange("p (c i j) -> p c j i", i=LINE, j=PACK),
-            w_raw[:].rearrange("p j (c i) -> p c j i", i=LINE),
+        nc.gpsimd.tensor_copy(
+            w_grouped[:, : W_CUT * PACK].rearrange("p (n j) -> p n j", j=PACK),
+            w_raw[:, :, :W_CUT].rearrange("p j n -> p n j"),
         )
+        nc.scalar.copy(
+            w_grouped[:, W_CUT * PACK :].rearrange("p (c i j) -> p c j i", i=LINE, j=PACK),
+            w_raw[:, :, W_CUT:].rearrange("p j (c i) -> p c j i", i=LINE),
+        )
+        cuts = [0, QUARTER, QUARTER + EIGHTH, HALF]
+        woven = [
+            reuse.tile([P, (b - a) * PACK], BF16, name=f"woven{a}", align_bytes=64, offset=8 * a)
+            for a, b in zip(cuts, cuts[1:])
+        ]
+        direct_codes = reuse.tile([P, HALF], U32, name="direct_codes", align_bytes=64, offset=2048)
+        words = pairs[:].bitcast(U32)
+        for tile, a, b in zip(woven, cuts, cuts[1:]):
+            nc.scalar.copy(
+                tile[:].bitcast(U32).rearrange("p (s u) -> p s u", u=2),
+                words[:, :, a:b].rearrange("p u s -> p s u"),
+            )
         w_codes = keep.tile([P, N], U32, name="w_codes", align_bytes=64)
         w_scales = keep.tile([P, N], U8, name="w_scales", align_bytes=64)
+        nc.vector.quantize_mx(out=w_codes[:].bitcast(FP8X4), scales=w_scales[:], in_=w_grouped[:])
 
-        first_codes = keep.tile([P, QUARTER], U32, name="first_codes", align_bytes=64)
-        later_codes = keep.tile([P, S], U32, name="later_codes", tag="w_then_codes", align_bytes=64)
+        woven_codes = keep.tile([P, HALF], U32, name="woven_codes", align_bytes=64)
         scores = keep.tile([P, S], F32, name="scores")
         for q in range(S // QUARTER):
-            h, first = divmod(q * QUARTER, HALF)
-            documents = slice(q * QUARTER, (q + 1) * QUARTER)
-            codes = later_codes[:, documents] if q else first_codes[:]
+            h, r = divmod(q, 2)
+            columns = slice(r * QUARTER, (r + 1) * QUARTER)
+            codes = (woven_codes if h else direct_codes)[:, columns]
             scales = keep.tile([P, QUARTER], U8, name=f"x_scales{q}", align_bytes=64)
-            nc.vector.quantize_mx(
-                out=codes.bitcast(FP8X4),
-                scales=scales[:],
-                in_=picked[h][:, first * PACK : (first + QUARTER) * PACK],
-            )
-            if q == 0:
-                nc.vector.quantize_mx(out=w_codes[:].bitcast(FP8X4), scales=w_scales[:], in_=w_grouped[:])
+            if not h:
+                sources = [direct[:, r * QUARTER * PACK : (r + 1) * QUARTER * PACK]]
+            else:
+                sources = [tile[:] for tile in (woven[1:] if r else woven[:1])]
+            width = QUARTER // len(sources)
+            for i, values in enumerate(sources):
+                part = slice(i * width, (i + 1) * width)
+                nc.vector.quantize_mx(out=codes[:, part].bitcast(FP8X4), scales=scales[:, part], in_=values)
             acc = psum.tile([P, QUARTER], F32, name=f"acc{q}")
             nc.tensor.matmul_mx(
                 out=acc[:],
@@ -100,7 +118,7 @@ def tile_picked_ranknet_sigmoid_e_kernel(tc, xT, w1, offs, win, lose, out):
                 start=True,
                 stop=True,
             )
-            nc.scalar.copy(scores[:, documents], acc[:])
+            nc.scalar.copy(scores[:, q * QUARTER : (q + 1) * QUARTER], acc[:])
 
         stores = [(0, STORE_CUT), (STORE_CUT, V)]
         steps = [[(0, STORE_CUT)], [(STORE_CUT, STEP_CUT), (STEP_CUT, V)]]

@@ -19,8 +19,6 @@ PACK = 4
 LANES = 16
 HALF = S // 2
 QUARTER = S // 4
-W_CUT = 56
-EIGHTH = S // 8
 LINE = 4
 STORE_CUT = V // 2
 STEP_CUT = 3 * V // 4
@@ -37,16 +35,21 @@ def tile_picked_ranknet_sigmoid_e_kernel(tc, xT, w1, offs, win, lose, out):
         win_sb = keep.tile([P, V // LANES], U16, name="win_sb")
         lose_sb = keep.tile([P, V // LANES], U16, name="lose_sb")
         planes = [keep.tile([P, T], F32, name=f"plane{j}") for j in range(PACK)]
-        w_raw = reuse.tile([P, PACK, N], F32, name="w_raw", align_bytes=64, offset=512)
+        w_raw = [
+            reuse.tile([P, 2, N], F32, name=f"w_raw{u}", align_bytes=64, offset=offset)
+            for u, offset in enumerate((512, 2048))
+        ]
 
         x_rows = xT.rearrange("(p j) t -> p j t", j=PACK)
-        for j in range(PACK):
-            cuts = [0, T // 2, 3 * T // 4, T] if j < PACK - 1 else [0, T]
+        pieces = [[0, T // 2, T], [0, T // 2, 3 * T // 4, T], [0, T // 2, 3 * T // 4, T], [0, T]]
+        for j, cuts in enumerate(pieces):
             for a, b in zip(cuts, cuts[1:]):
                 nc.sync.dma_start(planes[j][:, a:b], x_rows[:, j, a:b])
             if j == 0:
                 nc.sync.dma_start(offs_sb[:], offs)
-        nc.sync.dma_start(w_raw[:], w1.rearrange("(p j) n -> p j n", j=PACK))
+        w_rows = w1.rearrange("(p j) n -> p j n", j=PACK)
+        for u in range(2):
+            nc.sync.dma_start(w_raw[u][:], w_rows[:, 2 * u : 2 * u + 2, :])
         nc.sync.dma_start(win_sb[:], win)
         nc.sync.dma_start(lose_sb[:], lose)
 
@@ -69,25 +72,20 @@ def tile_picked_ranknet_sigmoid_e_kernel(tc, xT, w1, offs, win, lose, out):
             )
 
         w_grouped = keep.tile([P, N * PACK], BF16, name="w_grouped", align_bytes=64)
-        nc.gpsimd.tensor_copy(
-            w_grouped[:, : W_CUT * PACK].rearrange("p (n j) -> p n j", j=PACK),
-            w_raw[:, :, :W_CUT].rearrange("p j n -> p n j"),
-        )
-        nc.scalar.copy(
-            w_grouped[:, W_CUT * PACK :].rearrange("p (c i j) -> p c j i", i=LINE, j=PACK),
-            w_raw[:, :, W_CUT:].rearrange("p j (c i) -> p c j i", i=LINE),
-        )
-        cuts = [0, QUARTER, QUARTER + EIGHTH, HALF]
+        for u, copy in enumerate((nc.scalar.copy, nc.gpsimd.tensor_copy)):
+            copy(
+                w_grouped[:].rearrange("p (n u e) -> p n u e", u=2, e=2)[:, :, u, :],
+                w_raw[u][:].rearrange("p e n -> p n e"),
+            )
         woven = [
-            reuse.tile([P, (b - a) * PACK], BF16, name=f"woven{a}", align_bytes=64, offset=8 * a)
-            for a, b in zip(cuts, cuts[1:])
+            reuse.tile([P, QUARTER * PACK], BF16, name=f"woven{r}", align_bytes=64, offset=1024 * r) for r in range(2)
         ]
         direct_codes = reuse.tile([P, HALF], U32, name="direct_codes", align_bytes=64, offset=2048)
         words = pairs[:].bitcast(U32)
-        for tile, a, b in zip(woven, cuts, cuts[1:]):
+        for r in range(2):
             nc.scalar.copy(
-                tile[:].bitcast(U32).rearrange("p (s u) -> p s u", u=2),
-                words[:, :, a:b].rearrange("p u s -> p s u"),
+                woven[r][:].bitcast(U32).rearrange("p (s u) -> p s u", u=2),
+                words[:, :, r * QUARTER : (r + 1) * QUARTER].rearrange("p u s -> p s u"),
             )
         w_codes = keep.tile([P, N], U32, name="w_codes", align_bytes=64)
         w_scales = keep.tile([P, N], U8, name="w_scales", align_bytes=64)
@@ -99,15 +97,9 @@ def tile_picked_ranknet_sigmoid_e_kernel(tc, xT, w1, offs, win, lose, out):
             h, r = divmod(q, 2)
             columns = slice(r * QUARTER, (r + 1) * QUARTER)
             codes = (woven_codes if h else direct_codes)[:, columns]
+            values = woven[r][:] if h else direct[:, r * QUARTER * PACK : (r + 1) * QUARTER * PACK]
             scales = keep.tile([P, QUARTER], U8, name=f"x_scales{q}", align_bytes=64)
-            if not h:
-                sources = [direct[:, r * QUARTER * PACK : (r + 1) * QUARTER * PACK]]
-            else:
-                sources = [tile[:] for tile in (woven[1:] if r else woven[:1])]
-            width = QUARTER // len(sources)
-            for i, values in enumerate(sources):
-                part = slice(i * width, (i + 1) * width)
-                nc.vector.quantize_mx(out=codes[:, part].bitcast(FP8X4), scales=scales[:, part], in_=values)
+            nc.vector.quantize_mx(out=codes.bitcast(FP8X4), scales=scales[:], in_=values)
             acc = psum.tile([P, QUARTER], F32, name=f"acc{q}")
             nc.tensor.matmul_mx(
                 out=acc[:],

@@ -19,6 +19,9 @@ PACK = 4
 LANES = 16
 HALF = S // 2
 QUARTER = S // 4
+WORDS = 2 * QUARTER
+EDGE = 16
+OUTSIDE = WORDS - EDGE
 LINE = 4
 STORE_CUT = V // 2
 STEP_CUT = 3 * V // 4
@@ -35,10 +38,9 @@ def tile_picked_ranknet_sigmoid_e_kernel(tc, xT, w1, offs, win, lose, out):
         win_sb = keep.tile([P, V // LANES], U16, name="win_sb")
         lose_sb = keep.tile([P, V // LANES], U16, name="lose_sb")
         planes = [keep.tile([P, T], F32, name=f"plane{j}") for j in range(PACK)]
-        w_raw = [
-            reuse.tile([P, 2, N], F32, name=f"w_raw{u}", align_bytes=64, offset=offset)
-            for u, offset in enumerate((512, 2048))
-        ]
+        shared = keep.tile([P, 2 * OUTSIDE + 2 * N], F32, name="shared", align_bytes=64)
+        w_second = reuse.tile([P, 2, N], F32, name="w_second", align_bytes=64, offset=64)
+        w_raw = [shared[:, OUTSIDE : OUTSIDE + 2 * N].rearrange("p (e n) -> p e n", e=2), w_second[:]]
 
         x_rows = xT.rearrange("(p j) t -> p j t", j=PACK)
         pieces = [[0, T // 2, T], [0, T // 2, 3 * T // 4, T], [0, T // 2, 3 * T // 4, T], [0, T]]
@@ -49,7 +51,7 @@ def tile_picked_ranknet_sigmoid_e_kernel(tc, xT, w1, offs, win, lose, out):
                 nc.sync.dma_start(offs_sb[:], offs)
         w_rows = w1.rearrange("(p j) n -> p j n", j=PACK)
         for u in range(2):
-            nc.sync.dma_start(w_raw[u][:], w_rows[:, 2 * u : 2 * u + 2, :])
+            nc.sync.dma_start(w_raw[u], w_rows[:, 2 * u : 2 * u + 2, :])
         nc.sync.dma_start(win_sb[:], win)
         nc.sync.dma_start(lose_sb[:], lose)
 
@@ -72,19 +74,25 @@ def tile_picked_ranknet_sigmoid_e_kernel(tc, xT, w1, offs, win, lose, out):
             )
 
         w_grouped = keep.tile([P, N * PACK], BF16, name="w_grouped", align_bytes=64)
-        for u, copy in enumerate((nc.scalar.copy, nc.gpsimd.tensor_copy)):
-            copy(
-                w_grouped[:].rearrange("p (n u e) -> p n u e", u=2, e=2)[:, :, u, :],
-                w_raw[u][:].rearrange("p e n -> p n e"),
-            )
-        woven = [
-            reuse.tile([P, QUARTER * PACK], BF16, name=f"woven{r}", align_bytes=64, offset=1024 * r) for r in range(2)
+        shares = [
+            (nc.gpsimd.tensor_copy, 0, 0, EDGE),
+            (nc.scalar.copy, 0, EDGE, N),
+            (nc.gpsimd.tensor_copy, 1, 0, N),
         ]
-        direct_codes = reuse.tile([P, HALF], U32, name="direct_codes", align_bytes=64, offset=2048)
+        for copy, u, a, b in shares:
+            copy(
+                w_grouped[:].rearrange("p (n u e) -> p n u e", u=2, e=2)[:, a:b, u, :],
+                w_raw[u][:, :, a:b].rearrange("p e n -> p n e"),
+            )
+        woven = [shared[:, :WORDS].bitcast(BF16), shared[:, OUTSIDE + 2 * N - EDGE :].bitcast(BF16)]
+        woven_scales = [
+            reuse.tile([P, QUARTER], U8, name=f"woven_scales{r}", align_bytes=64, offset=QUARTER * r) for r in range(2)
+        ]
+        direct_codes = reuse.tile([P, HALF], U32, name="direct_codes", align_bytes=64, offset=1024)
         words = pairs[:].bitcast(U32)
         for r in range(2):
             nc.scalar.copy(
-                woven[r][:].bitcast(U32).rearrange("p (s u) -> p s u", u=2),
+                woven[r].bitcast(U32).rearrange("p (s u) -> p s u", u=2),
                 words[:, :, r * QUARTER : (r + 1) * QUARTER].rearrange("p u s -> p s u"),
             )
         w_codes = keep.tile([P, N], U32, name="w_codes", align_bytes=64)
@@ -93,12 +101,12 @@ def tile_picked_ranknet_sigmoid_e_kernel(tc, xT, w1, offs, win, lose, out):
 
         woven_codes = keep.tile([P, HALF], U32, name="woven_codes", align_bytes=64)
         scores = keep.tile([P, S], F32, name="scores")
-        for q in range(S // QUARTER):
+        for q in (2, 0, 1, 3):
             h, r = divmod(q, 2)
             columns = slice(r * QUARTER, (r + 1) * QUARTER)
             codes = (woven_codes if h else direct_codes)[:, columns]
-            values = woven[r][:] if h else direct[:, r * QUARTER * PACK : (r + 1) * QUARTER * PACK]
-            scales = keep.tile([P, QUARTER], U8, name=f"x_scales{q}", align_bytes=64)
+            values = woven[r] if h else direct[:, r * QUARTER * PACK : (r + 1) * QUARTER * PACK]
+            scales = keep.tile([P, QUARTER], U8, name=f"x_scales{q}", align_bytes=64) if not h else woven_scales[r]
             nc.vector.quantize_mx(out=codes.bitcast(FP8X4), scales=scales[:], in_=values)
             acc = psum.tile([P, QUARTER], F32, name=f"acc{q}")
             nc.tensor.matmul_mx(

@@ -21,7 +21,8 @@ HALF = S // 2
 QUARTER = S // 4
 WORDS = 2 * QUARTER
 EDGE = 16
-OUTSIDE = WORDS - EDGE
+OUTSIDE = QUARTER - EDGE
+EIGHTH = S // 8
 LINE = 4
 STORE_CUT = V // 2
 STEP_CUT = 3 * V // 4
@@ -38,7 +39,7 @@ def tile_picked_ranknet_sigmoid_e_kernel(tc, xT, w1, offs, win, lose, out):
         win_sb = keep.tile([P, V // LANES], U16, name="win_sb")
         lose_sb = keep.tile([P, V // LANES], U16, name="lose_sb")
         planes = [keep.tile([P, T], F32, name=f"plane{j}") for j in range(PACK)]
-        shared = keep.tile([P, 2 * OUTSIDE + 2 * N], F32, name="shared", align_bytes=64)
+        shared = keep.tile([P, QUARTER + 2 * N + WORDS - 2 * EDGE], F32, name="shared", align_bytes=64)
         w_second = reuse.tile([P, 2, N], F32, name="w_second", align_bytes=64, offset=64)
         w_raw = [shared[:, OUTSIDE : OUTSIDE + 2 * N].rearrange("p (e n) -> p e n", e=2), w_second[:]]
 
@@ -84,16 +85,21 @@ def tile_picked_ranknet_sigmoid_e_kernel(tc, xT, w1, offs, win, lose, out):
                 w_grouped[:].rearrange("p (n u e) -> p n u e", u=2, e=2)[:, a:b, u, :],
                 w_raw[u][:, :, a:b].rearrange("p e n -> p n e"),
             )
-        woven = [shared[:, :WORDS].bitcast(BF16), shared[:, OUTSIDE + 2 * N - EDGE :].bitcast(BF16)]
+        woven = [
+            shared[:, :QUARTER].bitcast(BF16),
+            shared[:, QUARTER : 2 * QUARTER].bitcast(BF16),
+            shared[:, OUTSIDE + 2 * N - EDGE :].bitcast(BF16),
+        ]
         woven_scales = [
             reuse.tile([P, QUARTER], U8, name=f"woven_scales{r}", align_bytes=64, offset=QUARTER * r) for r in range(2)
         ]
         direct_codes = reuse.tile([P, HALF], U32, name="direct_codes", align_bytes=64, offset=1024)
         words = pairs[:].bitcast(U32)
-        for r in range(2):
+        cuts = [0, EIGHTH, QUARTER, HALF]
+        for piece, a, b in zip(woven, cuts, cuts[1:]):
             nc.scalar.copy(
-                woven[r].bitcast(U32).rearrange("p (s u) -> p s u", u=2),
-                words[:, :, r * QUARTER : (r + 1) * QUARTER].rearrange("p u s -> p s u"),
+                piece.bitcast(U32).rearrange("p (s u) -> p s u", u=2),
+                words[:, :, a:b].rearrange("p u s -> p s u"),
             )
         w_codes = keep.tile([P, N], U32, name="w_codes", align_bytes=64)
         w_scales = keep.tile([P, N], U8, name="w_scales", align_bytes=64)
@@ -105,9 +111,15 @@ def tile_picked_ranknet_sigmoid_e_kernel(tc, xT, w1, offs, win, lose, out):
             h, r = divmod(q, 2)
             columns = slice(r * QUARTER, (r + 1) * QUARTER)
             codes = (woven_codes if h else direct_codes)[:, columns]
-            values = woven[r] if h else direct[:, r * QUARTER * PACK : (r + 1) * QUARTER * PACK]
+            if h:
+                sources = woven[2:] if r else woven[:2]
+            else:
+                sources = [direct[:, r * QUARTER * PACK : (r + 1) * QUARTER * PACK]]
             scales = keep.tile([P, QUARTER], U8, name=f"x_scales{q}", align_bytes=64) if not h else woven_scales[r]
-            nc.vector.quantize_mx(out=codes.bitcast(FP8X4), scales=scales[:], in_=values)
+            width = QUARTER // len(sources)
+            for i, values in enumerate(sources):
+                part = slice(i * width, (i + 1) * width)
+                nc.vector.quantize_mx(out=codes[:, part].bitcast(FP8X4), scales=scales[:, part], in_=values)
             acc = psum.tile([P, QUARTER], F32, name=f"acc{q}")
             nc.tensor.matmul_mx(
                 out=acc[:],

@@ -23,6 +23,7 @@ WORDS = 2 * QUARTER
 EDGE = 16
 OUTSIDE = QUARTER - EDGE
 EIGHTH = S // 8
+SLIVER = 128
 LINE = 4
 STORE_CUT = V // 2
 STEP_CUT = 3 * V // 4
@@ -44,10 +45,13 @@ def tile_picked_ranknet_sigmoid_e_kernel(tc, xT, w1, offs, win, lose, out):
         w_raw = [shared[:, OUTSIDE : OUTSIDE + 2 * N].rearrange("p (e n) -> p e n", e=2), w_second[:]]
 
         x_rows = xT.rearrange("(p j) t -> p j t", j=PACK)
-        pieces = [[0, T // 2, T], [0, T // 2, 3 * T // 4, T], [0, T // 2, 3 * T // 4, T], [0, T]]
-        for j, cuts in enumerate(pieces):
-            for a, b in zip(cuts, cuts[1:]):
-                nc.sync.dma_start(planes[j][:, a:b], x_rows[:, j, a:b])
+        for j in range(PACK):
+            wide = T - SLIVER if j == 2 else T
+            nc.sync.dma_start(planes[j][:, :wide], x_rows[:, j, :wide])
+            if j == 2:
+                cuts = [0, 32, 64, 96, 112, P]
+                for a, b in zip(cuts, cuts[1:]):
+                    nc.sync.dma_start(planes[j][a:b, wide:], x_rows[a:b, j, wide:])
             if j == 0:
                 nc.sync.dma_start(offs_sb[:], offs)
         w_rows = w1.rearrange("(p j) n -> p j n", j=PACK)

@@ -17,16 +17,11 @@ ALU = mybir.AluOpType
 P = 128
 PACK = 4
 LANES = 16
-HALF = S // 2
 QUARTER = S // 4
-WORDS = 2 * QUARTER
-EDGE = 16
-OUTSIDE = QUARTER - EDGE
+STEP = V // 4
 EIGHTH = S // 8
-SLIVER = 128
-LINE = 4
-STORE_CUT = V // 2
-STEP_CUT = 3 * V // 4
+W_CUT = 80
+DIRECT = 3 * QUARTER
 
 
 def tile_picked_ranknet_sigmoid_e_kernel(tc, xT, w1, offs, win, lose, out):
@@ -39,24 +34,20 @@ def tile_picked_ranknet_sigmoid_e_kernel(tc, xT, w1, offs, win, lose, out):
         offs_sb = keep.tile([P, S // LANES], U16, name="offs_sb")
         win_sb = keep.tile([P, V // LANES], U16, name="win_sb")
         lose_sb = keep.tile([P, V // LANES], U16, name="lose_sb")
-        planes = [keep.tile([P, T], F32, name=f"plane{j}") for j in range(PACK)]
-        shared = keep.tile([P, QUARTER + 2 * N + WORDS - 2 * EDGE], F32, name="shared", align_bytes=64)
-        w_second = reuse.tile([P, 2, N], F32, name="w_second", align_bytes=64, offset=64)
-        w_raw = [shared[:, OUTSIDE : OUTSIDE + 2 * N].rearrange("p (e n) -> p e n", e=2), w_second[:]]
+        first_planes = keep.tile([P, 2, T], F32, name="first_planes")
+        last_planes = [keep.tile([P, T], F32, name=f"plane{j}") for j in (2, 3)]
+        planes = [first_planes[:, 0, :], first_planes[:, 1, :], last_planes[0][:], last_planes[1][:]]
+        w_raw = reuse.tile([P, PACK, N], F32, name="w_raw", align_bytes=64, offset=0)
+
+        def entries(tile, a, b):
+            return tile[:, a // LANES : b // LANES]
 
         x_rows = xT.rearrange("(p j) t -> p j t", j=PACK)
-        for j in range(PACK):
-            wide = T - SLIVER if j == 2 else T
-            nc.sync.dma_start(planes[j][:, :wide], x_rows[:, j, :wide])
-            if j == 2:
-                cuts = [0, 32, 64, 96, 112, P]
-                for a, b in zip(cuts, cuts[1:]):
-                    nc.sync.dma_start(planes[j][a:b, wide:], x_rows[a:b, j, wide:])
-            if j == 0:
-                nc.sync.dma_start(offs_sb[:], offs)
-        w_rows = w1.rearrange("(p j) n -> p j n", j=PACK)
-        for u in range(2):
-            nc.sync.dma_start(w_raw[u], w_rows[:, 2 * u : 2 * u + 2, :])
+        nc.sync.dma_start(first_planes[:], x_rows[:, :2, :])
+        nc.sync.dma_start(offs_sb[:], offs)
+        for j in (2, 3):
+            nc.sync.dma_start(planes[j], x_rows[:, j, :])
+        nc.sync.dma_start(w_raw[:], w1.rearrange("(p j) n -> p j n", j=PACK))
         nc.sync.dma_start(win_sb[:], win)
         nc.sync.dma_start(lose_sb[:], lose)
 
@@ -65,87 +56,69 @@ def tile_picked_ranknet_sigmoid_e_kernel(tc, xT, w1, offs, win, lose, out):
         nc.vector.memset(warm_in[:], 0.0)
         nc.scalar.activation(warm_out[:], warm_in[:], ACT.Sigmoid)
 
-        direct = keep.tile([P, HALF * PACK], BF16, name="direct", align_bytes=64)
-        pairs = keep.tile([P, 2, HALF * 2], BF16, name="pairs")
-        first_half = offs_sb[:, : HALF // LANES]
-        second_half = offs_sb[:, HALF // LANES :]
+        direct = keep.tile([P, DIRECT * PACK], BF16, name="direct", align_bytes=64)
+        placed = keep.tile([P, QUARTER * PACK], BF16, name="placed", align_bytes=64)
+        flat = [[keep.tile([P, 2, EIGHTH], BF16 if u else F32, name=f"flat{u}{r}") for r in range(2)] for u in range(2)]
         for j in range(PACK):
             u, e = divmod(j, 2)
             nc.vector.tensor_copy(
-                pairs[:, u, :].rearrange("p (s e) -> p s e", e=2)[:, :, e], planes[j][:].indirect(second_half)
+                direct[:].rearrange("p (s j) -> p s j", j=PACK)[:, :, j], planes[j].indirect(entries(offs_sb, 0, DIRECT))
             )
-            nc.vector.tensor_copy(
-                direct[:].rearrange("p (s j) -> p s j", j=PACK)[:, :, j], planes[j][:].indirect(first_half)
-            )
+            for r in range(2):
+                a = DIRECT + r * EIGHTH
+                nc.scalar.activation(flat[u][r][:, e, :], planes[j].indirect(entries(offs_sb, a, a + EIGHTH)), ACT.Copy)
+            if e:
+                for r in range(2):
+                    nc.scalar.copy(
+                        placed[:].rearrange("p (s u e) -> p s u e", u=2, e=2)[:, r * EIGHTH : (r + 1) * EIGHTH, u, :],
+                        flat[u][r][:].rearrange("p e s -> p s e"),
+                    )
 
         w_grouped = keep.tile([P, N * PACK], BF16, name="w_grouped", align_bytes=64)
-        shares = [
-            (nc.gpsimd.tensor_copy, 0, 0, EDGE),
-            (nc.scalar.copy, 0, EDGE, N),
-            (nc.gpsimd.tensor_copy, 1, 0, N),
-        ]
-        for copy, u, a, b in shares:
+        for copy, a, b in ((nc.gpsimd.tensor_copy, 0, W_CUT), (nc.scalar.copy, W_CUT, N)):
             copy(
-                w_grouped[:].rearrange("p (n u e) -> p n u e", u=2, e=2)[:, a:b, u, :],
-                w_raw[u][:, :, a:b].rearrange("p e n -> p n e"),
+                w_grouped[:].rearrange("p (n j) -> p n j", j=PACK)[:, a:b, :],
+                w_raw[:, :, a:b].rearrange("p j n -> p n j"),
             )
-        woven = [
-            shared[:, :QUARTER].bitcast(BF16),
-            shared[:, QUARTER : 2 * QUARTER].bitcast(BF16),
-            shared[:, OUTSIDE + 2 * N - EDGE :].bitcast(BF16),
-        ]
-        woven_scales = [
-            reuse.tile([P, QUARTER], U8, name=f"woven_scales{r}", align_bytes=64, offset=QUARTER * r) for r in range(2)
-        ]
-        direct_codes = reuse.tile([P, HALF], U32, name="direct_codes", align_bytes=64, offset=1024)
-        words = pairs[:].bitcast(U32)
-        cuts = [0, EIGHTH, QUARTER, HALF]
-        for piece, a, b in zip(woven, cuts, cuts[1:]):
-            nc.scalar.copy(
-                piece.bitcast(U32).rearrange("p (s u) -> p s u", u=2),
-                words[:, :, a:b].rearrange("p u s -> p s u"),
-            )
+
         w_codes = keep.tile([P, N], U32, name="w_codes", align_bytes=64)
         w_scales = keep.tile([P, N], U8, name="w_scales", align_bytes=64)
-        nc.vector.quantize_mx(out=w_codes[:].bitcast(FP8X4), scales=w_scales[:], in_=w_grouped[:])
-
-        woven_codes = keep.tile([P, HALF], U32, name="woven_codes", align_bytes=64)
+        x_codes = keep.tile([P, S], U32, name="x_codes", align_bytes=64)
         scores = keep.tile([P, S], F32, name="scores")
-        for q in (2, 0, 1, 3):
-            h, r = divmod(q, 2)
-            columns = slice(r * QUARTER, (r + 1) * QUARTER)
-            codes = (woven_codes if h else direct_codes)[:, columns]
-            if h:
-                sources = woven[2:] if r else woven[:2]
+        for q in (3, 0, 1, 2):
+            columns = slice(q * QUARTER, (q + 1) * QUARTER)
+            values = placed[:] if q == 3 else direct[:, q * QUARTER * PACK : (q + 1) * QUARTER * PACK]
+            if q == 3:
+                scales = keep.tile([P, QUARTER], U8, name="placed_scales", align_bytes=64)
             else:
-                sources = [direct[:, r * QUARTER * PACK : (r + 1) * QUARTER * PACK]]
-            scales = keep.tile([P, QUARTER], U8, name=f"x_scales{q}", align_bytes=64) if not h else woven_scales[r]
-            width = QUARTER // len(sources)
-            for i, values in enumerate(sources):
-                part = slice(i * width, (i + 1) * width)
-                nc.vector.quantize_mx(out=codes[:, part].bitcast(FP8X4), scales=scales[:, part], in_=values)
+                scales = reuse.tile([P, QUARTER], U8, name=f"x_scales{q}", align_bytes=64, offset=QUARTER * q)
+            nc.vector.quantize_mx(out=x_codes[:, columns].bitcast(FP8X4), scales=scales[:], in_=values)
+            if q == 3:
+                nc.vector.quantize_mx(out=w_codes[:].bitcast(FP8X4), scales=w_scales[:], in_=w_grouped[:])
             acc = psum.tile([P, QUARTER], F32, name=f"acc{q}")
             nc.tensor.matmul_mx(
                 out=acc[:],
                 lhsT=w_codes[:].bitcast(FP8X4),
                 lhsT_scale=w_scales[:],
-                rhs=codes.bitcast(FP8X4),
+                rhs=x_codes[:, columns].bitcast(FP8X4),
                 rhs_scale=scales[:],
                 start=True,
                 stop=True,
             )
-            nc.scalar.copy(scores[:, q * QUARTER : (q + 1) * QUARTER], acc[:])
+            nc.scalar.copy(scores[:, columns], acc[:])
 
-        stores = [(0, STORE_CUT), (STORE_CUT, V)]
-        steps = [[(0, STORE_CUT)], [(STORE_CUT, STEP_CUT), (STEP_CUT, V)]]
         winners = keep.tile([P, V], F32, name="winners")
+        losers = keep.tile([P, V // 2], F32, name="losers")
         gaps = keep.tile([P, V], F32, name="gaps")
         probs = keep.tile([P, V], F32, name="probs")
-        for a, b in stores:
-            nc.vector.tensor_copy(winners[:, a:b], scores[:].indirect(win_sb[:, a // LANES : b // LANES]))
-        for (a, b), store_steps in zip(stores, steps):
-            for c, d in store_steps:
-                losers = scores[:].indirect(lose_sb[:, c // LANES : d // LANES])
-                nc.vector.tensor_tensor(gaps[:, c:d], losers, winners[:, c:d], ALU.subtract)
-                nc.scalar.activation(probs[:, c:d], gaps[:, c:d], ACT.Sigmoid, scale=-1.0)
-            nc.sync.dma_start(out[:, a:b], probs[:, a:b])
+        half = V // 2
+        nc.vector.tensor_copy(winners[:, :STEP], scores[:].indirect(entries(win_sb, 0, STEP)))
+        nc.scalar.activation(winners[:, STEP:half], scores[:].indirect(entries(win_sb, STEP, half)), ACT.Copy)
+        nc.vector.tensor_copy(losers[:], scores[:].indirect(entries(lose_sb, half, V)))
+        nc.scalar.activation(winners[:, half:], scores[:].indirect(entries(win_sb, half, V)), ACT.Copy)
+        for step in (1, 0, 2, 3):
+            a, b = step * STEP, (step + 1) * STEP
+            lost = scores[:].indirect(entries(lose_sb, a, b)) if a < half else losers[:, a - half : b - half]
+            nc.vector.tensor_tensor(gaps[:, a:b], lost, winners[:, a:b], ALU.subtract)
+            nc.scalar.activation(probs[:, a:b], gaps[:, a:b], ACT.Sigmoid, scale=-1.0)
+        nc.sync.dma_start(out, probs[:])

@@ -20,7 +20,8 @@ LANES = 16
 QUARTER = S // 4
 STEP = V // 4
 EIGHTH = S // 8
-W_CUT = 80
+LINE = 4
+W_CUT = 96
 DIRECT = 3 * QUARTER
 
 
@@ -75,11 +76,14 @@ def tile_picked_ranknet_sigmoid_e_kernel(tc, xT, w1, offs, win, lose, out):
                     )
 
         w_grouped = keep.tile([P, N * PACK], BF16, name="w_grouped", align_bytes=64)
-        for copy, a, b in ((nc.gpsimd.tensor_copy, 0, W_CUT), (nc.scalar.copy, W_CUT, N)):
-            copy(
-                w_grouped[:].rearrange("p (n j) -> p n j", j=PACK)[:, a:b, :],
-                w_raw[:, :, a:b].rearrange("p j n -> p n j"),
-            )
+        nc.gpsimd.tensor_copy(
+            w_grouped[:, : W_CUT * PACK].rearrange("p (n j) -> p n j", j=PACK),
+            w_raw[:, :, :W_CUT].rearrange("p j n -> p n j"),
+        )
+        nc.scalar.copy(
+            w_grouped[:, W_CUT * PACK :].rearrange("p (c i j) -> p c j i", i=LINE, j=PACK),
+            w_raw[:, :, W_CUT:].rearrange("p j (c i) -> p c j i", i=LINE),
+        )
 
         w_codes = keep.tile([P, N], U32, name="w_codes", align_bytes=64)
         w_scales = keep.tile([P, N], U8, name="w_scales", align_bytes=64)

@@ -19,10 +19,9 @@ PACK = 4
 LANES = 16
 QUARTER = S // 4
 STEP = V // 4
-EIGHTH = S // 8
 LINE = 4
-W_CUT = 96
-DIRECT = 3 * QUARTER
+W_CUT = 64
+SPLIT = 320
 
 
 def tile_picked_ranknet_sigmoid_e_kernel(tc, xT, w1, offs, win, lose, out):
@@ -57,23 +56,22 @@ def tile_picked_ranknet_sigmoid_e_kernel(tc, xT, w1, offs, win, lose, out):
         nc.vector.memset(warm_in[:], 0.0)
         nc.scalar.activation(warm_out[:], warm_in[:], ACT.Sigmoid)
 
-        direct = keep.tile([P, DIRECT * PACK], BF16, name="direct", align_bytes=64)
-        placed = keep.tile([P, QUARTER * PACK], BF16, name="placed", align_bytes=64)
-        flat = [[keep.tile([P, 2, EIGHTH], BF16 if u else F32, name=f"flat{u}{r}") for r in range(2)] for u in range(2)]
+        front = keep.tile([P, 3 * QUARTER * PACK], BF16, name="front", align_bytes=64)
+        back = keep.tile([P, QUARTER * PACK], BF16, name="back", align_bytes=64)
+        front_slots = front[:].rearrange("p (s j) -> p s j", j=PACK)
+        back_slots = back[:].rearrange("p (s j) -> p s j", j=PACK)
+        scalar_parts = ((back_slots, 3 * QUARTER, S), (front_slots[:, SPLIT:, :], SPLIT, 3 * QUARTER))
+        flat = keep.tile([P, 2, S - SPLIT], F32, name="flat")
         for j in range(PACK):
-            u, e = divmod(j, 2)
-            nc.vector.tensor_copy(
-                direct[:].rearrange("p (s j) -> p s j", j=PACK)[:, :, j], planes[j].indirect(entries(offs_sb, 0, DIRECT))
-            )
-            for r in range(2):
-                a = DIRECT + r * EIGHTH
-                nc.scalar.activation(flat[u][r][:, e, :], planes[j].indirect(entries(offs_sb, a, a + EIGHTH)), ACT.Copy)
-            if e:
-                for r in range(2):
-                    nc.scalar.copy(
-                        placed[:].rearrange("p (s u e) -> p s u e", u=2, e=2)[:, r * EIGHTH : (r + 1) * EIGHTH, u, :],
-                        flat[u][r][:].rearrange("p e s -> p s e"),
-                    )
+            nc.vector.tensor_copy(front_slots[:, :SPLIT, j], planes[j].indirect(entries(offs_sb, 0, SPLIT)))
+            if j < 2:
+                nc.scalar.activation(flat[:, j, :], planes[j].indirect(entries(offs_sb, SPLIT, S)), ACT.Copy)
+            else:
+                for slots, a, b in scalar_parts:
+                    nc.scalar.activation(slots[:, :, j], planes[j].indirect(entries(offs_sb, a, b)), ACT.Copy)
+            if j == 1:
+                for slots, a, b in scalar_parts:
+                    nc.scalar.copy(slots[:, :, :2], flat[:, :, a - SPLIT : b - SPLIT].rearrange("p e s -> p s e"))
 
         w_grouped = keep.tile([P, N * PACK], BF16, name="w_grouped", align_bytes=64)
         nc.gpsimd.tensor_copy(
@@ -91,9 +89,9 @@ def tile_picked_ranknet_sigmoid_e_kernel(tc, xT, w1, offs, win, lose, out):
         scores = keep.tile([P, S], F32, name="scores")
         for q in (3, 0, 1, 2):
             columns = slice(q * QUARTER, (q + 1) * QUARTER)
-            values = placed[:] if q == 3 else direct[:, q * QUARTER * PACK : (q + 1) * QUARTER * PACK]
+            values = back[:] if q == 3 else front[:, q * QUARTER * PACK : (q + 1) * QUARTER * PACK]
             if q == 3:
-                scales = keep.tile([P, QUARTER], U8, name="placed_scales", align_bytes=64)
+                scales = keep.tile([P, QUARTER], U8, name="back_scales", align_bytes=64)
             else:
                 scales = reuse.tile([P, QUARTER], U8, name=f"x_scales{q}", align_bytes=64, offset=QUARTER * q)
             nc.vector.quantize_mx(out=x_codes[:, columns].bitcast(FP8X4), scales=scales[:], in_=values)

@@ -20,7 +20,7 @@ LANES = 16
 QUARTER = S // 4
 STEP = V // 4
 LINE = 4
-W_CUT = 64
+W_CUT = 72
 SPLIT = 320
 
 
@@ -56,22 +56,15 @@ def tile_picked_ranknet_sigmoid_e_kernel(tc, xT, w1, offs, win, lose, out):
         nc.vector.memset(warm_in[:], 0.0)
         nc.scalar.activation(warm_out[:], warm_in[:], ACT.Sigmoid)
 
-        front = keep.tile([P, 3 * QUARTER * PACK], BF16, name="front", align_bytes=64)
-        back = keep.tile([P, QUARTER * PACK], BF16, name="back", align_bytes=64)
-        front_slots = front[:].rearrange("p (s j) -> p s j", j=PACK)
-        back_slots = back[:].rearrange("p (s j) -> p s j", j=PACK)
-        scalar_parts = ((back_slots, 3 * QUARTER, S), (front_slots[:, SPLIT:, :], SPLIT, 3 * QUARTER))
+        laid = keep.tile([P, S * PACK], BF16, name="laid", align_bytes=64)
+        slots = laid[:].rearrange("p (s j) -> p s j", j=PACK)
         flat = keep.tile([P, 2, S - SPLIT], F32, name="flat")
         for j in range(PACK):
-            nc.vector.tensor_copy(front_slots[:, :SPLIT, j], planes[j].indirect(entries(offs_sb, 0, SPLIT)))
-            if j < 2:
-                nc.scalar.activation(flat[:, j, :], planes[j].indirect(entries(offs_sb, SPLIT, S)), ACT.Copy)
-            else:
-                for slots, a, b in scalar_parts:
-                    nc.scalar.activation(slots[:, :, j], planes[j].indirect(entries(offs_sb, a, b)), ACT.Copy)
+            nc.vector.tensor_copy(slots[:, :SPLIT, j], planes[j].indirect(entries(offs_sb, 0, SPLIT)))
+            target = flat[:, j, :] if j < 2 else slots[:, SPLIT:, j]
+            nc.scalar.activation(target, planes[j].indirect(entries(offs_sb, SPLIT, S)), ACT.Copy)
             if j == 1:
-                for slots, a, b in scalar_parts:
-                    nc.scalar.copy(slots[:, :, :2], flat[:, :, a - SPLIT : b - SPLIT].rearrange("p e s -> p s e"))
+                nc.scalar.copy(slots[:, SPLIT:, :2], flat[:].rearrange("p e s -> p s e"))
 
         w_grouped = keep.tile([P, N * PACK], BF16, name="w_grouped", align_bytes=64)
         nc.gpsimd.tensor_copy(
@@ -89,7 +82,7 @@ def tile_picked_ranknet_sigmoid_e_kernel(tc, xT, w1, offs, win, lose, out):
         scores = keep.tile([P, S], F32, name="scores")
         for q in (3, 0, 1, 2):
             columns = slice(q * QUARTER, (q + 1) * QUARTER)
-            values = back[:] if q == 3 else front[:, q * QUARTER * PACK : (q + 1) * QUARTER * PACK]
+            values = laid[:, q * QUARTER * PACK : (q + 1) * QUARTER * PACK]
             if q == 3:
                 scales = keep.tile([P, QUARTER], U8, name="back_scales", align_bytes=64)
             else:

@@ -20,7 +20,7 @@ LANES = 16
 QUARTER = S // 4
 STEP = V // 4
 LINE = 4
-W_CUT = 72
+W_CUT = 80
 SPLIT = 320
 
 

@@ -100,7 +100,7 @@ def tile_picked_ranknet_sigmoid_e_kernel(tc, xT, w1, offs, win, lose, out):
                 start=True,
                 stop=True,
             )
-            nc.scalar.copy(scores[:, columns], acc[:])
+            nc.vector.tensor_copy(scores[:, columns], acc[:])
 
         winners = keep.tile([P, V], F32, name="winners")
         losers = keep.tile([P, V // 2], F32, name="losers")
@@ -110,8 +110,9 @@ def tile_picked_ranknet_sigmoid_e_kernel(tc, xT, w1, offs, win, lose, out):
         nc.vector.tensor_copy(winners[:, :STEP], scores[:].indirect(entries(win_sb, 0, STEP)))
         nc.scalar.activation(winners[:, STEP:half], scores[:].indirect(entries(win_sb, STEP, half)), ACT.Copy)
         nc.vector.tensor_copy(losers[:], scores[:].indirect(entries(lose_sb, half, V)))
-        nc.scalar.activation(winners[:, half:], scores[:].indirect(entries(win_sb, half, V)), ACT.Copy)
-        for step in (1, 0, 2, 3):
+        for a in (half, half + STEP):
+            nc.scalar.activation(winners[:, a : a + STEP], scores[:].indirect(entries(win_sb, a, a + STEP)), ACT.Copy)
+        for step in range(4):
             a, b = step * STEP, (step + 1) * STEP
             lost = scores[:].indirect(entries(lose_sb, a, b)) if a < half else losers[:, a - half : b - half]
             nc.vector.tensor_tensor(gaps[:, a:b], lost, winners[:, a:b], ALU.subtract)

from contextlib import ExitStack

import concourse.mybir as mybir

K, T, S, V, N = 512, 2048, 512, 256, 128
FLOPS = 2 * K * S * N

F32 = mybir.dt.float32
BF16 = mybir.dt.bfloat16
U32 = mybir.dt.uint32
U16 = mybir.dt.uint16
U8 = mybir.dt.uint8
FP8X4 = mybir.dt.float8_e4m3fn_x4
ACT = mybir.ActivationFunctionType
ALU = mybir.AluOpType

P = 128
PACK = 4
LANES = 16
QUARTER = S // 4
STEP = V // 4
LINE = 4
W_CUT = 80
SPLIT = 320


def tile_picked_ranknet_sigmoid_e_kernel(tc, xT, w1, offs, win, lose, out):
    nc = tc.nc
    with ExitStack() as ctx:
        keep = ctx.enter_context(tc.tile_pool(name="keep", bufs=1))
        reuse = ctx.enter_context(tc.tile_pool(name="reuse", bufs=1))
        psum = ctx.enter_context(tc.psum_pool(name="psum", bufs=1))

        offs_sb = keep.tile([P, S // LANES], U16, name="offs_sb")
        win_sb = keep.tile([P, V // LANES], U16, name="win_sb")
        lose_sb = keep.tile([P, V // LANES], U16, name="lose_sb")
        first_planes = keep.tile([P, 2, T], F32, name="first_planes")
        last_planes = [keep.tile([P, T], F32, name=f"plane{j}") for j in (2, 3)]
        planes = [first_planes[:, 0, :], first_planes[:, 1, :], last_planes[0][:], last_planes[1][:]]
        w_raw = reuse.tile([P, PACK, N], F32, name="w_raw", align_bytes=64, offset=0)

        def entries(tile, a, b):
            return tile[:, a // LANES : b // LANES]

        x_rows = xT.rearrange("(p j) t -> p j t", j=PACK)
        nc.sync.dma_start(first_planes[:], x_rows[:, :2, :])
        nc.sync.dma_start(offs_sb[:], offs)
        for j in (2, 3):
            nc.sync.dma_start(planes[j], x_rows[:, j, :])
        nc.sync.dma_start(w_raw[:], w1.rearrange("(p j) n -> p j n", j=PACK))
        nc.sync.dma_start(win_sb[:], win)
        nc.sync.dma_start(lose_sb[:], lose)

        warm_in = keep.tile([P, 1], F32, name="warm_in")
        warm_out = keep.tile([P, 1], F32, name="warm_out")
        nc.vector.memset(warm_in[:], 0.0)
        nc.scalar.activation(warm_out[:], warm_in[:], ACT.Sigmoid)

        laid = keep.tile([P, S * PACK], BF16, name="laid", align_bytes=64)
        slots = laid[:].rearrange("p (s j) -> p s j", j=PACK)
        flat = keep.tile([P, 2, S - SPLIT], F32, name="flat")
        for j in range(PACK):
            nc.vector.tensor_copy(slots[:, :SPLIT, j], planes[j].indirect(entries(offs_sb, 0, SPLIT)))
            target = flat[:, j, :] if j < 2 else slots[:, SPLIT:, j]
            nc.scalar.activation(target, planes[j].indirect(entries(offs_sb, SPLIT, S)), ACT.Copy)
            if j == 1:
                nc.scalar.copy(slots[:, SPLIT:, :2], flat[:].rearrange("p e s -> p s e"))

        w_grouped = keep.tile([P, N * PACK], BF16, name="w_grouped", align_bytes=64)
        nc.gpsimd.tensor_copy(
            w_grouped[:, : W_CUT * PACK].rearrange("p (n j) -> p n j", j=PACK),
            w_raw[:, :, :W_CUT].rearrange("p j n -> p n j"),
        )
        nc.scalar.copy(
            w_grouped[:, W_CUT * PACK :].rearrange("p (c i j) -> p c j i", i=LINE, j=PACK),
            w_raw[:, :, W_CUT:].rearrange("p j (c i) -> p c j i", i=LINE),
        )

        w_codes = keep.tile([P, N], U32, name="w_codes", align_bytes=64)
        w_scales = keep.tile([P, N], U8, name="w_scales", align_bytes=64)
        x_codes = keep.tile([P, S], U32, name="x_codes", align_bytes=64)
        scores = keep.tile([P, S], F32, name="scores")
        for q in (3, 0, 1, 2):
            columns = slice(q * QUARTER, (q + 1) * QUARTER)
            values = laid[:, q * QUARTER * PACK : (q + 1) * QUARTER * PACK]
            if q == 3:
                scales = keep.tile([P, QUARTER], U8, name="back_scales", align_bytes=64)
            else:
                scales = reuse.tile([P, QUARTER], U8, name=f"x_scales{q}", align_bytes=64, offset=QUARTER * q)
            nc.vector.quantize_mx(out=x_codes[:, columns].bitcast(FP8X4), scales=scales[:], in_=values)
            if q == 3:
                nc.vector.quantize_mx(out=w_codes[:].bitcast(FP8X4), scales=w_scales[:], in_=w_grouped[:])
            acc = psum.tile([P, QUARTER], F32, name=f"acc{q}")
            nc.tensor.matmul_mx(
                out=acc[:],
                lhsT=w_codes[:].bitcast(FP8X4),
                lhsT_scale=w_scales[:],
                rhs=x_codes[:, columns].bitcast(FP8X4),
                rhs_scale=scales[:],
                start=True,
                stop=True,
            )
            nc.vector.tensor_copy(scores[:, columns], acc[:])

        winners = keep.tile([P, V], F32, name="winners")
        losers = keep.tile([P, V // 2], F32, name="losers")
        gaps = keep.tile([P, V], F32, name="gaps")
        probs = keep.tile([P, V], F32, name="probs")
        half = V // 2
        nc.vector.tensor_copy(winners[:, :STEP], scores[:].indirect(entries(win_sb, 0, STEP)))
        nc.scalar.activation(winners[:, STEP:half], scores[:].indirect(entries(win_sb, STEP, half)), ACT.Copy)
        nc.vector.tensor_copy(losers[:], scores[:].indirect(entries(lose_sb, half, V)))
        for a in (half, half + STEP):
            nc.scalar.activation(winners[:, a : a + STEP], scores[:].indirect(entries(win_sb, a, a + STEP)), ACT.Copy)
        for step in range(4):
            a, b = step * STEP, (step + 1) * STEP
            lost = scores[:].indirect(entries(lose_sb, a, b)) if a < half else losers[:, a - half : b - half]
            nc.vector.tensor_tensor(gaps[:, a:b], lost, winners[:, a:b], ALU.subtract)
            nc.scalar.activation(probs[:, a:b], gaps[:, a:b], ACT.Sigmoid, scale=-1.0)
        nc.sync.dma_start(out, probs[:])
